import numpy as np
CORES = [0,1,2,3]
N = 4
ROOT = 1
def setup_inputs(rng):
    return {"x": rng.standard_normal((N, 128, 512), dtype=np.float32)}
def reference(x):
    y = np.full((N, 128, N * 512), np.nan, x.dtype)
    y[ROOT] = np.concatenate(list(x), axis=1)
    return {"y": y}

W = 512

SCRATCH = {
    "buf": ("sbuf", [128, 4 * W], "float32"),
}
SEMAPHORES = ["loaded", "sent", "arr0", "arr1", "arr2", "arr3", "stored", "gstored"]


def rank_program(g, core, T, topo):
    rank = T.rank_of(core)
    if rank is None:
        return
    n = len(T.cores)
    root = 1
    root_core = T.cores[root]

    if rank != root:
        blk = T.buf[:, rank * W:(rank + 1) * W]
        g.sync.dma_start(blk, T.x[:]).then_inc(T.sem.loaded, 16)
        g.wait_ge(T.sem.loaded, 16)
        rid, pid, _se = topo.addr(root_core)
        g.remote_dma(blk, blk, T.sem["arr%d" % rank], T.sem.sent, pid, rid, topo.mask(core, root_core))
        g.wait_ge(T.sem.sent, 16)
        return

    g.dma_start(T.y[:, root * W:(root + 1) * W], T.x[:]).then_inc(T.sem.gstored, 16)
    others = [j for j in range(n) if j != root]
    queues = [g.sync, g.scalar, g]
    for j, q in zip(others, queues):
        q.wait_ge(T.sem["arr%d" % j], 16)
        done = T.sem.gstored if q is g else T.sem.stored
        q.dma_start(T.y[:, j * W:(j + 1) * W], T.buf[:, j * W:(j + 1) * W]).then_inc(done, 16)
    g.wait_ge(T.sem.gstored, 32)
    g.wait_ge(T.sem.stored, 32)
